import numpy as np
import ml_dtypes


def mxq(x, axis, fmt="e4m3"):
    dtype, down = {"e4m3": (ml_dtypes.float8_e4m3fn, 7), "e5m2": (ml_dtypes.float8_e5m2, 14)}[fmt]
    v = np.moveaxis(np.asarray(x, np.float32).astype(ml_dtypes.bfloat16).astype(np.float64), axis, -1)
    blocks = v.reshape(v.shape[:-1] + (-1, 32))
    amax = np.abs(blocks).max(-1, keepdims=True)
    byte = np.maximum(np.where(amax > 0, np.frexp(amax)[1] - 1 + 127, 0) - down, 1)
    scale = np.exp2(byte - 127.0)
    codes = (blocks / scale).astype(np.float32).astype(dtype).astype(np.float64)
    return np.moveaxis((codes * scale).reshape(v.shape), -1, axis)


WIDE = False


def mx_kscale(k):
    if not WIDE:
        return np.ones(k)
    levels = np.array([10, -10, 5, -5, 0])
    if k % 512:
        return np.exp2(np.random.permutation(np.resize(levels, k // 32))).repeat(32)
    a = np.empty((k // 512, 16))
    for p in range(k // 512):
        a[p, :8] = np.random.permutation(np.resize(levels, 8))
        for g in range(8):
            far = levels[np.abs(levels - a[p, g]) >= 10]
            a[p, g + 8] = far[np.random.randint(len(far))]
    return np.exp2(a.ravel()).repeat(32)


BF16 = ml_dtypes.bfloat16


def bf(x):
    return np.asarray(x, np.float32).astype(BF16)


def f64(x):
    return np.asarray(x).astype(np.float64)


E2M1 = np.array([0.0, 0.5, 1.0, 1.5, 2.0, 3.0, 4.0, 6.0, -0.0, -0.5, -1.0, -1.5, -2.0, -3.0, -4.0, -6.0])


def pack_weight(w, fmt):
    k, n = w.shape
    w = f64(bf(w)).reshape(k // 32, 32, n)
    amax = np.abs(w).max(1)
    if fmt == "e4m3":
        byte = np.frexp(amax)[1] - 1 + 127 - 7
    else:
        mant, ex = np.frexp(amax / 6.0)
        byte = np.where(mant > 0.5, ex, ex - 1) + 127
    byte = np.clip(np.where(amax > 0, byte, 1), 1, 254)
    scaled = (w * np.exp2(127.0 - byte)[:, None, :]).reshape(k, n).astype(np.float32)
    by_word = np.ascontiguousarray(scaled.reshape(k // 512, 128, 4, n).transpose(0, 1, 3, 2))
    if fmt == "e4m3":
        words = by_word.astype(ml_dtypes.float8_e4m3fn).view(np.uint8)
    else:
        c = by_word.astype(ml_dtypes.float4_e2m1fn).view(np.uint8) & 0xF
        words = c[..., 0::2] | (c[..., 1::2] << 4)
    return np.ascontiguousarray(words), np.ascontiguousarray(byte.astype(np.uint8).reshape(k // 512, 16, n))


def unpack_weight(words, scales, fmt):
    g, p, n, _ = words.shape
    if fmt == "e4m3":
        vals = np.ascontiguousarray(words).view(ml_dtypes.float8_e4m3fn).astype(np.float64)
    else:
        nib = np.empty((g, p, n, 4), np.uint8)
        nib[..., 0::2] = words & 0xF
        nib[..., 1::2] = words >> 4
        vals = E2M1[nib]
    vals = vals * np.repeat(np.exp2(scales.astype(np.float64) - 127.0), 8, axis=1)[..., None]
    return vals.transpose(0, 1, 3, 2).reshape(g * 512, n)
def pack4(w):
    words, scales = pack_weight(w, "e2m1")
    return words.reshape(words.shape[0], 128, -1), scales


def unpack4(words, scales):
    return unpack_weight(words.reshape(words.shape[0], 128, -1, 2), scales, "e2m1")


def planes(Y):
    n, m = Y.shape
    b = f64(bf(Y)).reshape(n // 32, 32, m)
    amax = np.abs(b).max(1)
    byte = np.clip(np.where(amax > 0, np.frexp(amax)[1] - 1 + 127 - 7, 1), 1, 254)
    codes = (b * np.exp2(127.0 - byte)[:, None, :]).reshape(n, m).astype(np.float32).astype(ml_dtypes.float8_e4m3fn).view(np.uint8)
    words = codes.reshape(n // 512, 128, 4, m).transpose(0, 1, 3, 2)
    return np.ascontiguousarray(words), np.ascontiguousarray(byte.astype(np.uint8).reshape(n // 512, 16, m))


T, NA, NB, P, L, F, SNAP = 2048, 32, 32, 1024, 512, 1024, 8
WIDTH, FIELD = 2.0, 0.25

def cnoise(*shape):
    return np.random.randn(*shape) + 1j * np.random.randn(*shape)

def setup_inputs():
    pos_a, pos_b = L * np.random.rand(NA), L * np.random.rand(NB)
    ph_a, ph_b = 0.7 * np.random.randn(NA), 0.7 * np.random.randn(NB)
    u = FIELD * np.random.rand(T, 1)
    v = np.zeros((T, NA, NB), complex)
    for _ in range(SNAP):
        src = 0.35 * cnoise(T, 1)
        xa = (1.5 * cnoise(T, NA) + src * np.exp(1j * np.pi * u * pos_a)) * np.exp(1j * ph_a)
        xb = (1.5 * cnoise(T, NB) + src * np.exp(1j * np.pi * u * pos_b)) * np.exp(1j * ph_b)
        v = v + xb[:, None, :] * np.conj(xa)[:, :, None] / SNAP
    v = v.reshape(T, P)
    phase = (ph_b[None, :] - ph_a[:, None]).reshape(P, 1)
    dist = np.abs(pos_b[None, :] - pos_a[:, None]).reshape(P, 1)
    lag = np.arange(L)
    w = 1.0 / (1.0 + ((dist - lag) / WIDTH) ** 2)
    w = w / w.sum(axis=0)
    look = FIELD * (np.arange(F) + np.random.rand(F)) / F
    s1, s2, t = mx_kscale(P), mx_kscale(P), mx_kscale(L)
    avg_words, avg_scales = pack4(w * np.cos(phase) / s1[:, None])
    table = 4.0 * np.cos(np.pi * lag[:, None] * look) / np.sqrt(L)
    cos_words, cos_scales = pack_weight(table / t[:, None], "e4m3")
    return {"cov_re": bf(v.real * s1), "cov_im": bf(v.imag * s2),
            "avg_words": avg_words, "avg_scales": avg_scales,
            "quad": bf(w * np.sin(phase) / s2[:, None]),
            "offset": bf(0.1 * np.random.randn(L)),
            "taper": bf(np.exp(-lag / L) * (1 + 0.1 * np.random.randn(L)) * t),
            "cos_words": cos_words, "cos_scales": cos_scales,
            "level": bf(np.exp(0.3 * np.random.randn(T))),
            "floor": bf(0.3 * np.random.randn(F)),
            "gain": bf(np.exp(0.8 * np.random.randn(F)))}

def reference(cov_re, cov_im, avg_words, avg_scales, quad, offset, taper, cos_words, cos_scales, level, floor, gain):
    in_phase = mxq(f64(cov_re), 1, "e4m3") @ unpack4(avg_words, avg_scales)
    quadrature = mxq(f64(cov_im), 1, "e4m3") @ mxq(f64(quad), 0, "e4m3")
    h = (in_phase + quadrature + f64(offset)) * f64(taper)
    spec = mxq(h, 1, "e4m3") @ unpack_weight(cos_words, cos_scales, "e4m3")
    y = (spec * f64(level)[:, None] + f64(floor)) * f64(gain)
    words, scales = planes(y.T)
    return y, words, scales

@@ -1,0 +1,333 @@
+from contextlib import ExitStack
+
+import concourse.mybir as mybir
+from concourse.masks import make_identity
+
+T, K, L, F = 2048, 1024, 512, 1024
+FLOPS = 2 * T * (2 * K * L + L * F)
+
+F32 = mybir.dt.float32
+BF16 = mybir.dt.bfloat16
+I32 = mybir.dt.int32
+U32 = mybir.dt.uint32
+U8 = mybir.dt.uint8
+FP8X4 = mybir.dt.float8_e4m3fn_x4
+FP4X4 = mybir.dt.float4_e2m1fn_x4
+ALU = mybir.AluOpType
+ACT = mybir.ActivationFunctionType
+
+P = 128
+TILES = T // P
+LOOKAHEAD = 4
+
+
+def tile_coarray_lag_cosine_spectrum_k6_kernel(
+    tc, cov_re, cov_im, avg_words, avg_scales, quad, offset, taper, cos_words, cos_scales,
+    level, floor, gain, out_0, out_1, out_2,
+):
+    nc = tc.nc
+    with ExitStack() as ctx:
+        keep = ctx.enter_context(tc.tile_pool(name="keep", bufs=1))
+        loads = ctx.enter_context(tc.tile_pool(name="loads", bufs=6))
+        work = ctx.enter_context(tc.tile_pool(name="work", bufs=3))
+        psum = ctx.enter_context(tc.psum_pool(name="psum", bufs=8))
+        ctx.enter_context(tc.manual_schedule())
+
+        ident = keep.tile([P, P], F32)
+        level_rows = keep.tile([P, P], F32)
+        scale_raw = keep.tile([P, 2 * L + F], U8, align_bytes=64)
+        a_raw = keep.tile([P, 2, 2 * L], U8, align_bytes=64)
+        a_words = keep.tile([P, 2, 2 * L], U8, align_bytes=64)
+        a_scales = keep.tile([P, 2, L], U8, align_bytes=64)
+        q_raw = [keep.tile([P, 4, L], BF16, name="q_raw%d" % g) for g in range(2)]
+        q_grouped = [keep.tile([P, 4 * L], BF16, name="q_grouped%d" % g, align_bytes=64) for g in range(2)]
+        q_words = keep.tile([P, 2, L], U32, align_bytes=64)
+        q_scales = keep.tile([P, 2, L], U8, align_bytes=64)
+        c_words = keep.tile([P, F], U32, align_bytes=64)
+        offset_raw = keep.tile([P, 4], BF16)
+        taper_raw = keep.tile([P, 4], BF16)
+        floor_raw = keep.tile([P, 2, 4], BF16)
+        gain_raw = keep.tile([P, 2, 4], BF16)
+        level_raw = keep.tile([TILES, P], BF16)
+        taper_col = keep.tile([P, 4], F32)
+        bias_col = keep.tile([P, 4], F32)
+        floor_col = keep.tile([P, 8], F32)
+        gain_col = keep.tile([P, 8], F32)
+        level_col = keep.tile([P, TILES], F32)
+        floor_all = keep.tile([P, F], F32)
+        gain_all = keep.tile([P, F], F32)
+        y_words = keep.tile([P, 2, T], U32, align_bytes=64)
+        y_scales = keep.tile([P, 2, T], U8, align_bytes=64)
+        c_scales = scale_raw[:, 2 * L :]
+
+        cov_sb, cov_bank, cov_grouped, cov_q = {}, {}, {}, {}
+        h_bank, h_rows, h_grouped, h_q, s_bank = {}, {}, {}, {}, {}
+        shifted, y_sb, y_bf, y_bank, y_grouped = {}, {}, {}, {}, {}
+
+        def bank():
+            return psum.tile([P, 4, P], F32, name="bank")
+
+        def load_cov(i):
+            cov_sb[i] = []
+            for name, src in (("re", cov_re), ("im", cov_im)):
+                dst = loads.tile([P, K], BF16, name="rows_" + name)
+                nc.sync.dma_start(out=dst[:], in_=src[P * i : P * (i + 1), :])
+                cov_sb[i].append(dst)
+
+        def turn_cov(i):
+            cov_bank[i] = []
+            for src in cov_sb[i]:
+                words = src[:].bitcast(F32)
+                dst = bank()
+                for g in range(2):
+                    for u in range(2):
+                        nc.tensor.transpose(dst[:, 2 * g + u, :], words[:, 256 * g + u : 256 * (g + 1) : 2], ident[:])
+                cov_bank[i].append(dst)
+
+        def copy_cov(i):
+            grouped = work.tile([P, 2, 2, P, 4], BF16, name="cov_grouped", align_bytes=64)
+            cov_grouped[i] = grouped
+            for mat in range(2):
+                nc.scalar.copy(
+                    out=grouped[:, mat].bitcast(F32),
+                    in_=cov_bank[i][mat][:].rearrange("p (g u) m -> p g m u", u=2),
+                )
+
+        def quantize_cov(i):
+            words = work.tile([P, 4 * P], U32, name="cov_words", align_bytes=64)
+            scales = work.tile([P, 4 * P], U8, name="cov_scales", align_bytes=64)
+            cov_q[i] = (words, scales)
+            nc.vector.quantize_mx(
+                out=words[:].bitcast(FP8X4), scales=scales[:],
+                in_=cov_grouped[i][:].rearrange("p a g m t -> p (a g m t)"),
+            )
+
+        def stage1(i):
+            words, scales = cov_q[i]
+            dst = bank()
+            h_bank[i] = dst
+            for t in range(4):
+                cols = slice(P * t, P * (t + 1))
+                for c in range(4):
+                    g = c % 2
+                    if c < 2:
+                        lhsT = a_words[:, g, 2 * P * t : 2 * P * (t + 1)].bitcast(FP4X4)
+                        lhsT_scale = a_scales[:, g, cols]
+                    else:
+                        lhsT = q_words[:, g, cols].bitcast(FP8X4)
+                        lhsT_scale = q_scales[:, g, cols]
+                    nc.tensor.matmul_mx(
+                        out=dst[:, t, :], lhsT=lhsT, lhsT_scale=lhsT_scale,
+                        rhs=words[:, P * c : P * (c + 1)].bitcast(FP8X4), rhs_scale=scales[:, P * c : P * (c + 1)],
+                        start=(c == 0), stop=(c == 3),
+                    )
+
+        def taper_h(i):
+            rows = work.tile([P, 4, P], BF16, name="h_rows")
+            h_rows[i] = rows
+            for t in range(4):
+                nc.scalar.activation(
+                    out=rows[:, t, :], in_=h_bank[i][:, t, :], func=ACT.Identity,
+                    scale=taper_col[:, t : t + 1], bias=bias_col[:, t : t + 1],
+                )
+
+        def group_h(i):
+            grouped = work.tile([P, P, 4], BF16, name="h_grouped", align_bytes=64)
+            h_grouped[i] = grouped
+            nc.vector.tensor_copy(
+                out=grouped[:].rearrange("p (c i) t -> p c t i", i=4),
+                in_=h_rows[i][:].rearrange("p t (c i) -> p c t i", i=4),
+            )
+
+        def quantize_h(i):
+            words = work.tile([P, P], U32, name="h_words", align_bytes=64)
+            scales = work.tile([P, P], U8, name="h_scales", align_bytes=64)
+            h_q[i] = (words, scales)
+            nc.vector.quantize_mx(
+                out=words[:].bitcast(FP8X4), scales=scales[:], in_=h_grouped[i][:].rearrange("p m t -> p (m t)"),
+            )
+
+        def stage2(i):
+            words, scales = h_q[i]
+            s_bank[i] = []
+            for h in range(2):
+                cols = slice(512 * h, 512 * (h + 1))
+                dst = bank()
+                nc.tensor.matmul_mx(
+                    out=dst[:].rearrange("p a m -> p (a m)"),
+                    lhsT=words[:].bitcast(FP8X4), lhsT_scale=scales[:],
+                    rhs=c_words[:, cols].bitcast(FP8X4), rhs_scale=c_scales[:, cols],
+                    start=True, stop=True,
+                )
+                s_bank[i].append(dst)
+
+        def shift_s(i):
+            dst = work.tile([P, F], F32, name="shifted")
+            shifted[i] = dst
+            for h in range(2):
+                cols = slice(512 * h, 512 * (h + 1))
+                nc.vector.scalar_tensor_tensor(
+                    out=dst[:, cols], in0=s_bank[i][h][:].rearrange("p a m -> p (a m)"),
+                    scalar=level_col[:, i : i + 1], in1=floor_all[:, cols], op0=ALU.mult, op1=ALU.add,
+                )
+
+        def gain_y(i):
+            dst = loads.tile([P, F], F32, name="y_sb")
+            y_sb[i] = dst
+            nc.vector.tensor_tensor(out=dst[:], in0=shifted[i][:], in1=gain_all[:], op=ALU.mult)
+            nc.sync.dma_start(out=out_0[P * i : P * (i + 1), :], in_=dst[:])
+
+        def round_y(i):
+            dst = work.tile([P, 2, 2, P, 2], BF16, name="y_bf")
+            y_bf[i] = dst
+            nc.scalar.copy(out=dst[:], in_=y_sb[i][:].rearrange("m (g p u e) -> m g u p e", g=2, u=2, e=2))
+
+        def turn_y(i):
+            words = y_bf[i][:].rearrange("m g u p e -> m (g u) (p e)").bitcast(F32)
+            dst = bank()
+            y_bank[i] = dst
+            for c in range(4):
+                nc.tensor.transpose(dst[:, c, :], words[:, c, :], ident[:])
+
+        def copy_y(i):
+            if i % 2 == 0:
+                y_grouped[i // 2] = work.tile([P, 2, 2 * P, 4], BF16, name="y_grouped", align_bytes=64)
+            half = slice(P * (i % 2), P * (i % 2 + 1))
+            nc.scalar.copy(
+                out=y_grouped[i // 2][:, :, half, :].bitcast(F32),
+                in_=y_bank[i][:].rearrange("p (g u) m -> p g m u", u=2),
+            )
+
+        def quantize_y(pair):
+            cols = slice(2 * P * pair, 2 * P * (pair + 1))
+            for g in range(2):
+                nc.vector.quantize_mx(
+                    out=y_words[:, g, cols].bitcast(FP8X4), scales=y_scales[:, g, cols],
+                    in_=y_grouped[pair][:, g].rearrange("p m t -> p (m t)"),
+                )
+            nc.sync.dma_start(
+                out=out_1.rearrange("g p m t -> p g (m t)").bitcast(I32)[:, :, cols],
+                in_=y_words[:, :, cols].bitcast(I32),
+            )
+
+        def store_scales(first, last):
+            for q in range(4):
+                nc.sync.dma_start(
+                    out=out_2[:, 4 * q : 4 * q + 4, first:last].rearrange("g r m -> r g m").bitcast(I32),
+                    in_=y_scales[32 * q : 32 * q + 4, :, first:last].bitcast(I32),
+                )
+
+        def load_quad(g):
+            nc.sync.dma_start(out=q_raw[g][:], in_=quad[512 * g : 512 * (g + 1), :].rearrange("(p j) c -> p j c", j=4))
+
+        def group_quad(g, copy):
+            copy(
+                out=q_grouped[g][:].rearrange("p (t m j) -> p t m j", t=4, j=4),
+                in_=q_raw[g][:].rearrange("p j (m t) -> p t m j", t=4),
+            )
+
+        def quantize_quad(g):
+            nc.vector.quantize_mx(out=q_words[:, g, :].bitcast(FP8X4), scales=q_scales[:, g, :], in_=q_grouped[g][:])
+
+        def spread(col, dst):
+            for h in range(2):
+                turned = bank()
+                for j in range(4):
+                    c = 4 * h + j
+                    nc.tensor.transpose(turned[:, j, :], col[:, c : c + 1].to_broadcast([P, P]), ident[:])
+                nc.scalar.copy(
+                    out=dst[:, 512 * h : 512 * (h + 1)].rearrange("p (n j) -> p n j", j=4),
+                    in_=turned[:].rearrange("p j n -> p n j"),
+                )
+
+        make_identity(nc, ident[:])
+        nc.gpsimd.memset(level_rows[:], 0.0)
+        nc.vector.memset(scale_raw[:].bitcast(I32), 0)
+        load_cov(0)
+        load_quad(0)
+        nc.sync.dma_start(out=a_raw[:].bitcast(I32), in_=avg_words.rearrange("g p b -> p g b").bitcast(I32))
+        for q in range(4):
+            nc.sync.dma_start(
+                out=scale_raw[32 * q : 32 * q + 4, : 2 * L].rearrange("r (g n) -> r g n", g=2).bitcast(I32),
+                in_=avg_scales[:, 4 * q : 4 * q + 4, :].rearrange("g r n -> r g n").bitcast(I32),
+            )
+        load_quad(1)
+        nc.sync.dma_start(out=offset_raw[:], in_=offset.rearrange("(p t) -> p t", t=4))
+        nc.sync.dma_start(out=taper_raw[:], in_=taper.rearrange("(p t) -> p t", t=4))
+        load_cov(1)
+        nc.sync.dma_start(out=floor_raw[:], in_=floor.rearrange("(h n j) -> n h j", h=2, j=4))
+        nc.sync.dma_start(out=gain_raw[:], in_=gain.rearrange("(h n j) -> n h j", h=2, j=4))
+        nc.sync.dma_start(out=level_raw[:], in_=level.rearrange("(i m) -> i m", m=P))
+        nc.sync.dma_start(out=c_words[:].bitcast(I32), in_=cos_words[0].rearrange("p n t -> p (n t)").bitcast(I32))
+        for q in range(4):
+            nc.sync.dma_start(
+                out=scale_raw[32 * q : 32 * q + 4, 2 * L :].bitcast(I32),
+                in_=cos_scales[0, 4 * q : 4 * q + 4, :].bitcast(I32),
+            )
+        for i in range(2, LOOKAHEAD):
+            load_cov(i)
+
+        turn_cov(0)
+        copy_cov(0)
+        group_quad(0, nc.vector.tensor_copy)
+        nc.vector.tensor_copy(
+            out=a_words[:].rearrange("p g (t m b) -> p g t m b", t=4, b=2),
+            in_=a_raw[:].rearrange("p g (m t b) -> p g t m b", t=4, b=2),
+        )
+        quantize_quad(0)
+        quantize_cov(0)
+        group_quad(1, nc.scalar.copy)
+        nc.vector.tensor_copy(
+            out=a_scales[:].rearrange("p g (t m) -> p g t m", t=4),
+            in_=scale_raw[:, : 2 * L].rearrange("p (g m t) -> p g t m", g=2, t=4),
+        )
+        nc.vector.tensor_copy(out=floor_col[:], in_=floor_raw[:].rearrange("p h j -> p (h j)"))
+        nc.vector.tensor_copy(out=gain_col[:], in_=gain_raw[:].rearrange("p h j -> p (h j)"))
+        nc.vector.tensor_copy(out=level_rows[:TILES, :], in_=level_raw[:])
+        nc.vector.tensor_copy(out=taper_col[:], in_=taper_raw[:])
+        nc.vector.tensor_tensor(out=bias_col[:], in0=offset_raw[:], in1=taper_raw[:], op=ALU.mult)
+        quantize_quad(1)
+
+        def live(i):
+            return 0 <= i < TILES
+
+        for s in range(1, TILES + 4):
+            if live(s + LOOKAHEAD - 1):
+                load_cov(s + LOOKAHEAD - 1)
+            if live(s - 3):
+                shift_s(s - 3)
+            if live(s - 2):
+                taper_h(s - 2)
+            if live(s):
+                turn_cov(s)
+            if live(s - 4):
+                turn_y(s - 4)
+            if live(s):
+                copy_cov(s)
+            if live(s - 4):
+                copy_y(s - 4)
+            if live(s - 2):
+                group_h(s - 2)
+            if live(s - 3):
+                gain_y(s - 3)
+                round_y(s - 3)
+            if live(s - 1):
+                stage1(s - 1)
+            if s == 1:
+                turned = bank()
+                nc.tensor.transpose(turned[:, 0, :], level_rows[:], ident[:])
+                nc.scalar.copy(out=level_col[:], in_=turned[:, 0, :TILES])
+                spread(floor_col, floor_all)
+            if s == 2:
+                spread(gain_col, gain_all)
+            if live(s - 2):
+                quantize_h(s - 2)
+                stage2(s - 2)
+            if live(s):
+                quantize_cov(s)
+            if live(s - 4) and s % 2 == 1:
+                quantize_y((s - 4) // 2)
+                if s - 4 == TILES - 3:
+                    store_scales(0, T - 2 * P)
+                if s - 4 == TILES - 1:
+                    store_scales(T - 2 * P, T)

@@ -3,8 +3,8 @@ from contextlib import ExitStack
 import concourse.mybir as mybir
 from concourse.masks import make_identity
 
-T, K, L, F = 2048, 1024, 512, 1024
-FLOPS = 2 * T * (2 * K * L + L * F)
+WINDOWS, PAIRS, LAGS, DIRS = 2048, 1024, 512, 1024
+FLOPS = 2 * WINDOWS * (2 * PAIRS * LAGS + LAGS * DIRS)
 
 F32 = mybir.dt.float32
 BF16 = mybir.dt.bfloat16
@@ -17,8 +17,14 @@ ALU = mybir.AluOpType
 ACT = mybir.ActivationFunctionType
 
 P = 128
-TILES = T // P
-LOOKAHEAD = 4
+PACK = 4
+GROUP = P * PACK
+TILES = WINDOWS // P
+LAST = TILES - 1
+BOTH, HALVES = [(0, 2)], [(0, 1), (1, 2)]
+
+H_GROUPED_ON_SCALAR = {0, 13, 14, 15}
+EARLY_SCALES = 1536
 
 
 def tile_coarray_lag_cosine_spectrum_k6_kernel(
@@ -28,130 +34,174 @@ def tile_coarray_lag_cosine_spectrum_k6_kernel(
     nc = tc.nc
     with ExitStack() as ctx:
         keep = ctx.enter_context(tc.tile_pool(name="keep", bufs=1))
-        loads = ctx.enter_context(tc.tile_pool(name="loads", bufs=6))
         work = ctx.enter_context(tc.tile_pool(name="work", bufs=3))
         psum = ctx.enter_context(tc.psum_pool(name="psum", bufs=8))
         ctx.enter_context(tc.manual_schedule())
 
         ident = keep.tile([P, P], F32)
         level_rows = keep.tile([P, P], F32)
-        scale_raw = keep.tile([P, 2 * L + F], U8, align_bytes=64)
-        a_raw = keep.tile([P, 2, 2 * L], U8, align_bytes=64)
-        a_words = keep.tile([P, 2, 2 * L], U8, align_bytes=64)
-        a_scales = keep.tile([P, 2, L], U8, align_bytes=64)
-        q_raw = [keep.tile([P, 4, L], BF16, name="q_raw%d" % g) for g in range(2)]
-        q_grouped = [keep.tile([P, 4 * L], BF16, name="q_grouped%d" % g, align_bytes=64) for g in range(2)]
-        q_words = keep.tile([P, 2, L], U32, align_bytes=64)
-        q_scales = keep.tile([P, 2, L], U8, align_bytes=64)
-        c_words = keep.tile([P, F], U32, align_bytes=64)
-        offset_raw = keep.tile([P, 4], BF16)
-        taper_raw = keep.tile([P, 4], BF16)
-        floor_raw = keep.tile([P, 2, 4], BF16)
-        gain_raw = keep.tile([P, 2, 4], BF16)
-        level_raw = keep.tile([TILES, P], BF16)
-        taper_col = keep.tile([P, 4], F32)
-        bias_col = keep.tile([P, 4], F32)
-        floor_col = keep.tile([P, 8], F32)
-        gain_col = keep.tile([P, 8], F32)
+        scales_in = keep.tile([P, 2 * LAGS + DIRS], U8, align_bytes=64)
+        a_in = keep.tile([P, 2, 2 * LAGS], U8, align_bytes=64)
+        a_words = keep.tile([P, 2, 2 * LAGS], U8, align_bytes=64)
+        a_scales = keep.tile([P, 2, LAGS], U8, align_bytes=64)
+        quad_in = [keep.tile([P, PACK, LAGS], BF16, name="quad_in%d" % g) for g in range(2)]
+        quad_grouped = [
+            keep.tile([P, PACK * LAGS], BF16, name="quad_grouped%d" % g, align_bytes=64) for g in range(2)
+        ]
+        quad_words = keep.tile([P, 2, LAGS], U32, align_bytes=64)
+        quad_scales = keep.tile([P, 2, LAGS], U8, align_bytes=64)
+        c_words = keep.tile([P, DIRS], U32, align_bytes=64)
+        offset_in = keep.tile([P, PACK], BF16)
+        taper_in = keep.tile([P, PACK], BF16)
+        floor_in = keep.tile([P, DIRS // P], BF16)
+        gain_in = keep.tile([P, DIRS // P], BF16)
+        level_in = keep.tile([TILES, P], BF16)
+        taper_col = keep.tile([P, PACK], F32)
+        bias_col = keep.tile([P, PACK], F32)
         level_col = keep.tile([P, TILES], F32)
-        floor_all = keep.tile([P, F], F32)
-        gain_all = keep.tile([P, F], F32)
-        y_words = keep.tile([P, 2, T], U32, align_bytes=64)
-        y_scales = keep.tile([P, 2, T], U8, align_bytes=64)
-        c_scales = scale_raw[:, 2 * L :]
+        floor_all = keep.tile([P, DIRS], BF16)
+        gain_all = keep.tile([P, DIRS], BF16)
+        y_words = keep.tile([P, 2, WINDOWS], U32, align_bytes=64)
+        y_scales = keep.tile([P, 2, WINDOWS], U8, align_bytes=64)
+        c_scales = scales_in[:, 2 * LAGS :]
 
-        cov_sb, cov_bank, cov_grouped, cov_q = {}, {}, {}, {}
-        h_bank, h_rows, h_grouped, h_q, s_bank = {}, {}, {}, {}, {}
-        shifted, y_sb, y_bf, y_bank, y_grouped = {}, {}, {}, {}, {}
+        cov_rows, cov_banks, cov_grouped, cov_mx = {}, {}, {}, {}
+        h_bank, h_rows, h_grouped, h_mx, s_banks = {}, {}, {}, {}, {}
+        shifted, y_f32, y_bf16, y_bank, y_grouped = {}, {}, {}, {}, {}
 
         def bank():
             return psum.tile([P, 4, P], F32, name="bank")
 
+
+        def load_scale_rows(dst, src):
+            for q in range(4):
+                nc.sync.dma_start(
+                    out=dst[32 * q : 32 * q + 4, :].rearrange("r (g n) -> r g n", g=src.shape[0]).bitcast(I32),
+                    in_=src[:, 4 * q : 4 * q + 4, :].rearrange("g r n -> r g n").bitcast(I32),
+                )
+
+        def load_quad(g):
+            rows = quad[GROUP * g : GROUP * (g + 1), :]
+            nc.sync.dma_start(out=quad_in[g][:], in_=rows.rearrange("(p j) c -> p j c", j=PACK))
+
+        def group_quad(g, copy):
+            copy(
+                out=quad_grouped[g][:].rearrange("p (t m j) -> p t m j", t=PACK, j=PACK),
+                in_=quad_in[g][:].rearrange("p j (m t) -> p t m j", t=PACK),
+            )
+
+        def quantize_quad(g):
+            nc.vector.quantize_mx(
+                out=quad_words[:, g, :].bitcast(FP8X4), scales=quad_scales[:, g, :], in_=quad_grouped[g][:]
+            )
+
+        def order_a_words():
+            nc.vector.tensor_copy(
+                out=a_words[:].rearrange("p g (t m b) -> p g t m b", t=PACK, b=2),
+                in_=a_in[:].rearrange("p g (m t b) -> p g t m b", t=PACK, b=2),
+            )
+
+        def order_a_scales():
+            nc.vector.tensor_copy(
+                out=a_scales[:].rearrange("p g (t m) -> p g t m", t=PACK),
+                in_=scales_in[:, : 2 * LAGS].rearrange("p (g m t) -> p g t m", g=2, t=PACK),
+            )
+
+        def turn_vector(src):
+            words = src[:].bitcast(F32)
+            dst = bank()
+            for c in range(4):
+                nc.tensor.transpose(dst[:, c, :], words[:, c : c + 1].to_broadcast([P, P]), ident[:])
+            return dst
+
+        def copy_vector(dst, turned, copy):
+            copy(
+                out=dst[:].bitcast(F32).rearrange("p (n c) -> p n c", c=4),
+                in_=turned[:].rearrange("p c n -> p n c"),
+            )
+
+
         def load_cov(i):
-            cov_sb[i] = []
-            for name, src in (("re", cov_re), ("im", cov_im)):
-                dst = loads.tile([P, K], BF16, name="rows_" + name)
-                nc.sync.dma_start(out=dst[:], in_=src[P * i : P * (i + 1), :])
-                cov_sb[i].append(dst)
+            cov_rows[i] = work.tile([P, 4, GROUP], BF16, name="cov_rows", bufs=10)
+            for mat, src in enumerate((cov_re, cov_im)):
+                nc.sync.dma_start(
+                    out=cov_rows[i][:, 2 * mat : 2 * mat + 2, :].rearrange("m g k -> m (g k)"),
+                    in_=src[P * i : P * (i + 1), :],
+                )
 
         def turn_cov(i):
-            cov_bank[i] = []
-            for src in cov_sb[i]:
-                words = src[:].bitcast(F32)
+            words = cov_rows[i][:].bitcast(F32)
+            cov_banks[i] = []
+            for mat in range(2):
                 dst = bank()
                 for g in range(2):
                     for u in range(2):
-                        nc.tensor.transpose(dst[:, 2 * g + u, :], words[:, 256 * g + u : 256 * (g + 1) : 2], ident[:])
-                cov_bank[i].append(dst)
+                        nc.tensor.transpose(dst[:, 2 * g + u, :], words[:, 2 * mat + g, u : 2 * P : 2], ident[:])
+                cov_banks[i].append(dst)
 
         def copy_cov(i):
-            grouped = work.tile([P, 2, 2, P, 4], BF16, name="cov_grouped", align_bytes=64)
-            cov_grouped[i] = grouped
+            cov_grouped[i] = work.tile([P, 2, 2, P, PACK], BF16, name="cov_grouped", align_bytes=64)
             for mat in range(2):
                 nc.scalar.copy(
-                    out=grouped[:, mat].bitcast(F32),
-                    in_=cov_bank[i][mat][:].rearrange("p (g u) m -> p g m u", u=2),
+                    out=cov_grouped[i][:, mat].bitcast(F32),
+                    in_=cov_banks[i][mat][:].rearrange("p (g u) m -> p g m u", u=2),
                 )
 
         def quantize_cov(i):
-            words = work.tile([P, 4 * P], U32, name="cov_words", align_bytes=64)
-            scales = work.tile([P, 4 * P], U8, name="cov_scales", align_bytes=64)
-            cov_q[i] = (words, scales)
+            words = work.tile([P, 4 * P], U32, name="cov_words", bufs=6, align_bytes=64)
+            scales = work.tile([P, 4 * P], U8, name="cov_scales", bufs=6, align_bytes=64)
+            cov_mx[i] = (words, scales)
             nc.vector.quantize_mx(
                 out=words[:].bitcast(FP8X4), scales=scales[:],
                 in_=cov_grouped[i][:].rearrange("p a g m t -> p (a g m t)"),
             )
 
         def stage1(i):
-            words, scales = cov_q[i]
-            dst = bank()
-            h_bank[i] = dst
-            for t in range(4):
+            words, scales = cov_mx[i]
+            h_bank[i] = bank()
+            for t in range(PACK):
                 cols = slice(P * t, P * (t + 1))
                 for c in range(4):
-                    g = c % 2
-                    if c < 2:
+                    mat, g = divmod(c, 2)
+                    part = slice(P * c, P * (c + 1))
+                    if mat == 0:
                         lhsT = a_words[:, g, 2 * P * t : 2 * P * (t + 1)].bitcast(FP4X4)
                         lhsT_scale = a_scales[:, g, cols]
                     else:
-                        lhsT = q_words[:, g, cols].bitcast(FP8X4)
-                        lhsT_scale = q_scales[:, g, cols]
+                        lhsT = quad_words[:, g, cols].bitcast(FP8X4)
+                        lhsT_scale = quad_scales[:, g, cols]
                     nc.tensor.matmul_mx(
-                        out=dst[:, t, :], lhsT=lhsT, lhsT_scale=lhsT_scale,
-                        rhs=words[:, P * c : P * (c + 1)].bitcast(FP8X4), rhs_scale=scales[:, P * c : P * (c + 1)],
+                        out=h_bank[i][:, t, :], lhsT=lhsT, lhsT_scale=lhsT_scale,
+                        rhs=words[:, part].bitcast(FP8X4), rhs_scale=scales[:, part],
                         start=(c == 0), stop=(c == 3),
                     )
 
         def taper_h(i):
-            rows = work.tile([P, 4, P], BF16, name="h_rows")
-            h_rows[i] = rows
-            for t in range(4):
+            h_rows[i] = work.tile([P, PACK, P], BF16, name="h_rows", bufs=4)
+            for t in range(PACK):
                 nc.scalar.activation(
-                    out=rows[:, t, :], in_=h_bank[i][:, t, :], func=ACT.Identity,
+                    out=h_rows[i][:, t, :], in_=h_bank[i][:, t, :], func=ACT.Identity,
                     scale=taper_col[:, t : t + 1], bias=bias_col[:, t : t + 1],
                 )
 
         def group_h(i):
-            grouped = work.tile([P, P, 4], BF16, name="h_grouped", align_bytes=64)
-            h_grouped[i] = grouped
-            nc.vector.tensor_copy(
-                out=grouped[:].rearrange("p (c i) t -> p c t i", i=4),
-                in_=h_rows[i][:].rearrange("p t (c i) -> p c t i", i=4),
-            )
+            copy = nc.scalar.copy if i in H_GROUPED_ON_SCALAR else nc.vector.tensor_copy
+            h_grouped[i] = work.tile([P, P, PACK], BF16, name="h_grouped", bufs=4, align_bytes=64)
+            copy(out=h_grouped[i][:], in_=h_rows[i][:].rearrange("p t m -> p m t"))
 
         def quantize_h(i):
-            words = work.tile([P, P], U32, name="h_words", align_bytes=64)
-            scales = work.tile([P, P], U8, name="h_scales", align_bytes=64)
-            h_q[i] = (words, scales)
+            words = work.tile([P, P], U32, name="h_words", bufs=4, align_bytes=64)
+            scales = work.tile([P, P], U8, name="h_scales", bufs=4, align_bytes=64)
+            h_mx[i] = (words, scales)
             nc.vector.quantize_mx(
-                out=words[:].bitcast(FP8X4), scales=scales[:], in_=h_grouped[i][:].rearrange("p m t -> p (m t)"),
+                out=words[:].bitcast(FP8X4), scales=scales[:], in_=h_grouped[i][:].rearrange("p m t -> p (m t)")
             )
 
         def stage2(i):
-            words, scales = h_q[i]
-            s_bank[i] = []
-            for h in range(2):
-                cols = slice(512 * h, 512 * (h + 1))
+            words, scales = h_mx[i]
+            s_banks[i] = []
+            for g in range(2):
+                cols = slice(GROUP * g, GROUP * (g + 1))
                 dst = bank()
                 nc.tensor.matmul_mx(
                     out=dst[:].rearrange("p a m -> p (a m)"),
@@ -159,175 +209,142 @@ def tile_coarray_lag_cosine_spectrum_k6_kernel(
                     rhs=c_words[:, cols].bitcast(FP8X4), rhs_scale=c_scales[:, cols],
                     start=True, stop=True,
                 )
-                s_bank[i].append(dst)
+                s_banks[i].append(dst)
 
         def shift_s(i):
-            dst = work.tile([P, F], F32, name="shifted")
-            shifted[i] = dst
-            for h in range(2):
-                cols = slice(512 * h, 512 * (h + 1))
+            shifted[i] = work.tile([P, DIRS], F32, name="shifted")
+            for g in range(2):
+                cols = slice(GROUP * g, GROUP * (g + 1))
                 nc.vector.scalar_tensor_tensor(
-                    out=dst[:, cols], in0=s_bank[i][h][:].rearrange("p a m -> p (a m)"),
+                    out=shifted[i][:, cols], in0=s_banks[i][g][:].rearrange("p a m -> p (a m)"),
                     scalar=level_col[:, i : i + 1], in1=floor_all[:, cols], op0=ALU.mult, op1=ALU.add,
                 )
 
+        def parts(i):
+            return HALVES if i == LAST else BOTH
+
         def gain_y(i):
-            dst = loads.tile([P, F], F32, name="y_sb")
-            y_sb[i] = dst
-            nc.vector.tensor_tensor(out=dst[:], in0=shifted[i][:], in1=gain_all[:], op=ALU.mult)
-            nc.sync.dma_start(out=out_0[P * i : P * (i + 1), :], in_=dst[:])
+            y_f32[i] = work.tile([P, DIRS], F32, name="y_f32", bufs=6)
+            for lo, hi in parts(i):
+                cols = slice(GROUP * lo, GROUP * hi)
+                nc.vector.tensor_tensor(
+                    out=y_f32[i][:, cols], in0=shifted[i][:, cols], in1=gain_all[:, cols], op=ALU.mult
+                )
+                nc.sync.dma_start(out=out_0[P * i : P * (i + 1), cols], in_=y_f32[i][:, cols])
 
         def round_y(i):
-            dst = work.tile([P, 2, 2, P, 2], BF16, name="y_bf")
-            y_bf[i] = dst
-            nc.scalar.copy(out=dst[:], in_=y_sb[i][:].rearrange("m (g p u e) -> m g u p e", g=2, u=2, e=2))
+            copy = nc.vector.tensor_copy if i == LAST else nc.scalar.copy
+            y_bf16[i] = work.tile([P, 2, 2 * P, 2], BF16, name="y_bf16", bufs=4)
+            src = y_f32[i][:].rearrange("m (w u e) -> m u w e", u=2, e=2)
+            for lo, hi in parts(i):
+                copy(out=y_bf16[i][:, :, P * lo : P * hi, :], in_=src[:, :, P * lo : P * hi, :])
 
         def turn_y(i):
-            words = y_bf[i][:].rearrange("m g u p e -> m (g u) (p e)").bitcast(F32)
-            dst = bank()
-            y_bank[i] = dst
-            for c in range(4):
-                nc.tensor.transpose(dst[:, c, :], words[:, c, :], ident[:])
+            words = y_bf16[i][:].rearrange("m u w e -> m u (w e)").bitcast(F32)
+            for lo, hi in parts(i):
+                y_bank[i, lo] = bank()
+                for g in range(lo, hi):
+                    for u in range(2):
+                        nc.tensor.transpose(
+                            y_bank[i, lo][:, 2 * g + u, :], words[:, u, P * g : P * (g + 1)], ident[:]
+                        )
 
         def copy_y(i):
             if i % 2 == 0:
-                y_grouped[i // 2] = work.tile([P, 2, 2 * P, 4], BF16, name="y_grouped", align_bytes=64)
-            half = slice(P * (i % 2), P * (i % 2 + 1))
-            nc.scalar.copy(
-                out=y_grouped[i // 2][:, :, half, :].bitcast(F32),
-                in_=y_bank[i][:].rearrange("p (g u) m -> p g m u", u=2),
-            )
-
-        def quantize_y(pair):
-            cols = slice(2 * P * pair, 2 * P * (pair + 1))
-            for g in range(2):
-                nc.vector.quantize_mx(
-                    out=y_words[:, g, cols].bitcast(FP8X4), scales=y_scales[:, g, cols],
-                    in_=y_grouped[pair][:, g].rearrange("p m t -> p (m t)"),
+                y_grouped[i // 2] = work.tile([P, 2, 2 * P, PACK], BF16, name="y_grouped", align_bytes=64)
+            windows = slice(P * (i % 2), P * (i % 2 + 1))
+            for lo, hi in parts(i):
+                nc.scalar.copy(
+                    out=y_grouped[i // 2][:, lo:hi, windows, :].bitcast(F32),
+                    in_=y_bank[i, lo][:, 2 * lo : 2 * hi, :].rearrange("p (g u) m -> p g m u", u=2),
                 )
-            nc.sync.dma_start(
-                out=out_1.rearrange("g p m t -> p g (m t)").bitcast(I32)[:, :, cols],
-                in_=y_words[:, :, cols].bitcast(I32),
-            )
 
-        def store_scales(first, last):
+        def store_scales(first, last, queues):
             for q in range(4):
-                nc.sync.dma_start(
+                queues[q % len(queues)].dma_start(
                     out=out_2[:, 4 * q : 4 * q + 4, first:last].rearrange("g r m -> r g m").bitcast(I32),
                     in_=y_scales[32 * q : 32 * q + 4, :, first:last].bitcast(I32),
                 )
 
-        def load_quad(g):
-            nc.sync.dma_start(out=q_raw[g][:], in_=quad[512 * g : 512 * (g + 1), :].rearrange("(p j) c -> p j c", j=4))
-
-        def group_quad(g, copy):
-            copy(
-                out=q_grouped[g][:].rearrange("p (t m j) -> p t m j", t=4, j=4),
-                in_=q_raw[g][:].rearrange("p j (m t) -> p t m j", t=4),
-            )
-
-        def quantize_quad(g):
-            nc.vector.quantize_mx(out=q_words[:, g, :].bitcast(FP8X4), scales=q_scales[:, g, :], in_=q_grouped[g][:])
-
-        def spread(col, dst):
-            for h in range(2):
-                turned = bank()
-                for j in range(4):
-                    c = 4 * h + j
-                    nc.tensor.transpose(turned[:, j, :], col[:, c : c + 1].to_broadcast([P, P]), ident[:])
-                nc.scalar.copy(
-                    out=dst[:, 512 * h : 512 * (h + 1)].rearrange("p (n j) -> p n j", j=4),
-                    in_=turned[:].rearrange("p j n -> p n j"),
+        def quantize_y(i):
+            if i % 2 == 0:
+                return
+            windows = slice(P * (i - 1), P * (i + 1))
+            for lo, hi in parts(i):
+                for g in range(lo, hi):
+                    nc.vector.quantize_mx(
+                        out=y_words[:, g, windows].bitcast(FP8X4), scales=y_scales[:, g, windows],
+                        in_=y_grouped[i // 2][:, g].rearrange("p m t -> p (m t)"),
+                    )
+                nc.sync.dma_start(
+                    out=out_1.rearrange("g p m t -> p g (m t)").bitcast(I32)[:, lo:hi, windows],
+                    in_=y_words[:, lo:hi, windows].bitcast(I32),
                 )
+            if windows.stop == EARLY_SCALES:
+                store_scales(0, EARLY_SCALES, [nc.sync])
+            if i == LAST:
+                store_scales(EARLY_SCALES, WINDOWS, [nc.sync, nc.scalar])
+
 
         make_identity(nc, ident[:])
         nc.gpsimd.memset(level_rows[:], 0.0)
-        nc.vector.memset(scale_raw[:].bitcast(I32), 0)
-        load_cov(0)
-        load_quad(0)
-        nc.sync.dma_start(out=a_raw[:].bitcast(I32), in_=avg_words.rearrange("g p b -> p g b").bitcast(I32))
-        for q in range(4):
-            nc.sync.dma_start(
-                out=scale_raw[32 * q : 32 * q + 4, : 2 * L].rearrange("r (g n) -> r g n", g=2).bitcast(I32),
-                in_=avg_scales[:, 4 * q : 4 * q + 4, :].rearrange("g r n -> r g n").bitcast(I32),
-            )
-        load_quad(1)
-        nc.sync.dma_start(out=offset_raw[:], in_=offset.rearrange("(p t) -> p t", t=4))
-        nc.sync.dma_start(out=taper_raw[:], in_=taper.rearrange("(p t) -> p t", t=4))
-        load_cov(1)
-        nc.sync.dma_start(out=floor_raw[:], in_=floor.rearrange("(h n j) -> n h j", h=2, j=4))
-        nc.sync.dma_start(out=gain_raw[:], in_=gain.rearrange("(h n j) -> n h j", h=2, j=4))
-        nc.sync.dma_start(out=level_raw[:], in_=level.rearrange("(i m) -> i m", m=P))
-        nc.sync.dma_start(out=c_words[:].bitcast(I32), in_=cos_words[0].rearrange("p n t -> p (n t)").bitcast(I32))
-        for q in range(4):
-            nc.sync.dma_start(
-                out=scale_raw[32 * q : 32 * q + 4, 2 * L :].bitcast(I32),
-                in_=cos_scales[0, 4 * q : 4 * q + 4, :].bitcast(I32),
-            )
-        for i in range(2, LOOKAHEAD):
-            load_cov(i)
+        nc.vector.memset(scales_in[:].bitcast(I32), 0)
 
+        load_cov(0)
+        load_scale_rows(scales_in[:, : 2 * LAGS], avg_scales)
+        load_quad(0)
+        load_quad(1)
+        nc.sync.dma_start(out=floor_in[:], in_=floor.rearrange("(n j) -> n j", n=P))
+        nc.sync.dma_start(out=gain_in[:], in_=gain.rearrange("(n j) -> n j", n=P))
+        nc.sync.dma_start(out=a_in[:].bitcast(I32), in_=avg_words.rearrange("g p b -> p g b").bitcast(I32))
+        nc.sync.dma_start(out=taper_in[:], in_=taper.rearrange("(p t) -> p t", t=PACK))
+        load_cov(1)
+        nc.sync.dma_start(out=level_in[:], in_=level.rearrange("(i m) -> i m", m=P))
+        load_cov(2)
+        nc.sync.dma_start(out=offset_in[:], in_=offset.rearrange("(p t) -> p t", t=PACK))
+        load_cov(3)
+        load_cov(4)
+
+        order_a_scales()
         turn_cov(0)
         copy_cov(0)
         group_quad(0, nc.vector.tensor_copy)
-        nc.vector.tensor_copy(
-            out=a_words[:].rearrange("p g (t m b) -> p g t m b", t=4, b=2),
-            in_=a_raw[:].rearrange("p g (m t b) -> p g t m b", t=4, b=2),
-        )
-        quantize_quad(0)
         quantize_cov(0)
+        floor_turned = turn_vector(floor_in)
+        quantize_quad(0)
+        order_a_words()
         group_quad(1, nc.scalar.copy)
-        nc.vector.tensor_copy(
-            out=a_scales[:].rearrange("p g (t m) -> p g t m", t=4),
-            in_=scale_raw[:, : 2 * L].rearrange("p (g m t) -> p g t m", g=2, t=4),
-        )
-        nc.vector.tensor_copy(out=floor_col[:], in_=floor_raw[:].rearrange("p h j -> p (h j)"))
-        nc.vector.tensor_copy(out=gain_col[:], in_=gain_raw[:].rearrange("p h j -> p (h j)"))
-        nc.vector.tensor_copy(out=level_rows[:TILES, :], in_=level_raw[:])
-        nc.vector.tensor_copy(out=taper_col[:], in_=taper_raw[:])
-        nc.vector.tensor_tensor(out=bias_col[:], in0=offset_raw[:], in1=taper_raw[:], op=ALU.mult)
+        gain_turned = turn_vector(gain_in)
         quantize_quad(1)
+        copy_vector(floor_all, floor_turned, nc.vector.tensor_copy)
+        nc.vector.tensor_copy(out=taper_col[:], in_=taper_in[:])
+        nc.vector.tensor_tensor(out=bias_col[:], in0=offset_in[:], in1=taper_in[:], op=ALU.mult)
 
-        def live(i):
-            return 0 <= i < TILES
+        def finish_gain():
+            copy_vector(gain_all, gain_turned, nc.scalar.copy)
+            nc.vector.tensor_copy(out=level_rows[:TILES, :], in_=level_in[:])
 
-        for s in range(1, TILES + 4):
-            if live(s + LOOKAHEAD - 1):
-                load_cov(s + LOOKAHEAD - 1)
-            if live(s - 3):
-                shift_s(s - 3)
-            if live(s - 2):
-                taper_h(s - 2)
-            if live(s):
-                turn_cov(s)
-            if live(s - 4):
-                turn_y(s - 4)
-            if live(s):
-                copy_cov(s)
-            if live(s - 4):
-                copy_y(s - 4)
-            if live(s - 2):
-                group_h(s - 2)
-            if live(s - 3):
-                gain_y(s - 3)
-                round_y(s - 3)
-            if live(s - 1):
-                stage1(s - 1)
-            if s == 1:
-                turned = bank()
-                nc.tensor.transpose(turned[:, 0, :], level_rows[:], ident[:])
-                nc.scalar.copy(out=level_col[:], in_=turned[:, 0, :TILES])
-                spread(floor_col, floor_all)
-            if s == 2:
-                spread(gain_col, gain_all)
-            if live(s - 2):
-                quantize_h(s - 2)
-                stage2(s - 2)
-            if live(s):
-                quantize_cov(s)
-            if live(s - 4) and s % 2 == 1:
-                quantize_y((s - 4) // 2)
-                if s - 4 == TILES - 3:
-                    store_scales(0, T - 2 * P)
-                if s - 4 == TILES - 1:
-                    store_scales(T - 2 * P, T)
+        def load_c():
+            nc.sync.dma_start(
+                out=c_words[:].bitcast(I32), in_=cos_words[0].rearrange("p n t -> p (n t)").bitcast(I32)
+            )
+            load_scale_rows(c_scales, cos_scales)
+
+        def turn_level():
+            turned = bank()
+            nc.tensor.transpose(turned[:, 0, :], level_rows[:], ident[:])
+            nc.scalar.copy(out=level_col[:], in_=turned[:, 0, :TILES])
+
+        stages = [
+            (round_y, -4), (load_cov, 5), (turn_y, -5), (taper_h, -1), (turn_cov, 1), (quantize_y, -6),
+            (stage2, -2), (group_h, -1), (stage1, 0), (copy_cov, 1), (shift_s, -2), (quantize_h, -1),
+            (quantize_cov, 1), (copy_y, -5), (gain_y, -2),
+        ]
+        once = {(0, quantize_cov): finish_gain, (1, turn_cov): load_c, (2, turn_cov): turn_level}
+        steps = TILES - min(lead for stage, lead in stages)
+        for s in range(steps):
+            for stage, lead in stages:
+                if 0 <= s + lead < TILES:
+                    stage(s + lead)
+                if (s, stage) in once:
+                    once[s, stage]()

from contextlib import ExitStack

import concourse.mybir as mybir
from concourse.masks import make_identity

WINDOWS, PAIRS, LAGS, DIRS = 2048, 1024, 512, 1024
FLOPS = 2 * WINDOWS * (2 * PAIRS * LAGS + LAGS * DIRS)

F32 = mybir.dt.float32
BF16 = mybir.dt.bfloat16
I32 = mybir.dt.int32
U32 = mybir.dt.uint32
U8 = mybir.dt.uint8
FP8X4 = mybir.dt.float8_e4m3fn_x4
FP4X4 = mybir.dt.float4_e2m1fn_x4
ALU = mybir.AluOpType
ACT = mybir.ActivationFunctionType

P = 128
PACK = 4
GROUP = P * PACK
TILES = WINDOWS // P
LAST = TILES - 1
BOTH, HALVES = [(0, 2)], [(0, 1), (1, 2)]

H_GROUPED_ON_SCALAR = {0, 13, 14, 15}
EARLY_SCALES = 1536


def tile_coarray_lag_cosine_spectrum_k6_kernel(
    tc, cov_re, cov_im, avg_words, avg_scales, quad, offset, taper, cos_words, cos_scales,
    level, floor, gain, out_0, out_1, out_2,
):
    nc = tc.nc
    with ExitStack() as ctx:
        keep = ctx.enter_context(tc.tile_pool(name="keep", bufs=1))
        work = ctx.enter_context(tc.tile_pool(name="work", bufs=3))
        psum = ctx.enter_context(tc.psum_pool(name="psum", bufs=8))
        ctx.enter_context(tc.manual_schedule())

        ident = keep.tile([P, P], F32)
        level_rows = keep.tile([P, P], F32)
        scales_in = keep.tile([P, 2 * LAGS + DIRS], U8, align_bytes=64)
        a_in = keep.tile([P, 2, 2 * LAGS], U8, align_bytes=64)
        a_words = keep.tile([P, 2, 2 * LAGS], U8, align_bytes=64)
        a_scales = keep.tile([P, 2, LAGS], U8, align_bytes=64)
        quad_in = [keep.tile([P, PACK, LAGS], BF16, name="quad_in%d" % g) for g in range(2)]
        quad_grouped = [
            keep.tile([P, PACK * LAGS], BF16, name="quad_grouped%d" % g, align_bytes=64) for g in range(2)
        ]
        quad_words = keep.tile([P, 2, LAGS], U32, align_bytes=64)
        quad_scales = keep.tile([P, 2, LAGS], U8, align_bytes=64)
        c_words = keep.tile([P, DIRS], U32, align_bytes=64)
        offset_in = keep.tile([P, PACK], BF16)
        taper_in = keep.tile([P, PACK], BF16)
        floor_in = keep.tile([P, DIRS // P], BF16)
        gain_in = keep.tile([P, DIRS // P], BF16)
        level_in = keep.tile([TILES, P], BF16)
        taper_col = keep.tile([P, PACK], F32)
        bias_col = keep.tile([P, PACK], F32)
        level_col = keep.tile([P, TILES], F32)
        floor_all = keep.tile([P, DIRS], BF16)
        gain_all = keep.tile([P, DIRS], BF16)
        y_words = keep.tile([P, 2, WINDOWS], U32, align_bytes=64)
        y_scales = keep.tile([P, 2, WINDOWS], U8, align_bytes=64)
        c_scales = scales_in[:, 2 * LAGS :]

        cov_rows, cov_banks, cov_grouped, cov_mx = {}, {}, {}, {}
        h_bank, h_rows, h_grouped, h_mx, s_banks = {}, {}, {}, {}, {}
        shifted, y_f32, y_bf16, y_bank, y_grouped = {}, {}, {}, {}, {}

        def bank():
            return psum.tile([P, 4, P], F32, name="bank")


        def load_scale_rows(dst, src):
            for q in range(4):
                nc.sync.dma_start(
                    out=dst[32 * q : 32 * q + 4, :].rearrange("r (g n) -> r g n", g=src.shape[0]).bitcast(I32),
                    in_=src[:, 4 * q : 4 * q + 4, :].rearrange("g r n -> r g n").bitcast(I32),
                )

        def load_quad(g):
            rows = quad[GROUP * g : GROUP * (g + 1), :]
            nc.sync.dma_start(out=quad_in[g][:], in_=rows.rearrange("(p j) c -> p j c", j=PACK))

        def group_quad(g, copy):
            copy(
                out=quad_grouped[g][:].rearrange("p (t m j) -> p t m j", t=PACK, j=PACK),
                in_=quad_in[g][:].rearrange("p j (m t) -> p t m j", t=PACK),
            )

        def quantize_quad(g):
            nc.vector.quantize_mx(
                out=quad_words[:, g, :].bitcast(FP8X4), scales=quad_scales[:, g, :], in_=quad_grouped[g][:]
            )

        def order_a_words():
            nc.vector.tensor_copy(
                out=a_words[:].rearrange("p g (t m b) -> p g t m b", t=PACK, b=2),
                in_=a_in[:].rearrange("p g (m t b) -> p g t m b", t=PACK, b=2),
            )

        def order_a_scales():
            nc.vector.tensor_copy(
                out=a_scales[:].rearrange("p g (t m) -> p g t m", t=PACK),
                in_=scales_in[:, : 2 * LAGS].rearrange("p (g m t) -> p g t m", g=2, t=PACK),
            )

        def turn_vector(src):
            words = src[:].bitcast(F32)
            dst = bank()
            for c in range(4):
                nc.tensor.transpose(dst[:, c, :], words[:, c : c + 1].to_broadcast([P, P]), ident[:])
            return dst

        def copy_vector(dst, turned, copy):
            copy(
                out=dst[:].bitcast(F32).rearrange("p (n c) -> p n c", c=4),
                in_=turned[:].rearrange("p c n -> p n c"),
            )


        def load_cov(i):
            cov_rows[i] = work.tile([P, 4, GROUP], BF16, name="cov_rows", bufs=10)
            for mat, src in enumerate((cov_re, cov_im)):
                nc.sync.dma_start(
                    out=cov_rows[i][:, 2 * mat : 2 * mat + 2, :].rearrange("m g k -> m (g k)"),
                    in_=src[P * i : P * (i + 1), :],
                )

        def turn_cov(i):
            words = cov_rows[i][:].bitcast(F32)
            cov_banks[i] = []
            for mat in range(2):
                dst = bank()
                for g in range(2):
                    for u in range(2):
                        nc.tensor.transpose(dst[:, 2 * g + u, :], words[:, 2 * mat + g, u : 2 * P : 2], ident[:])
                cov_banks[i].append(dst)

        def copy_cov(i):
            cov_grouped[i] = work.tile([P, 2, 2, P, PACK], BF16, name="cov_grouped", align_bytes=64)
            for mat in range(2):
                nc.scalar.copy(
                    out=cov_grouped[i][:, mat].bitcast(F32),
                    in_=cov_banks[i][mat][:].rearrange("p (g u) m -> p g m u", u=2),
                )

        def quantize_cov(i):
            words = work.tile([P, 4 * P], U32, name="cov_words", bufs=6, align_bytes=64)
            scales = work.tile([P, 4 * P], U8, name="cov_scales", bufs=6, align_bytes=64)
            cov_mx[i] = (words, scales)
            nc.vector.quantize_mx(
                out=words[:].bitcast(FP8X4), scales=scales[:],
                in_=cov_grouped[i][:].rearrange("p a g m t -> p (a g m t)"),
            )

        def stage1(i):
            words, scales = cov_mx[i]
            h_bank[i] = bank()
            for t in range(PACK):
                cols = slice(P * t, P * (t + 1))
                for c in range(4):
                    mat, g = divmod(c, 2)
                    part = slice(P * c, P * (c + 1))
                    if mat == 0:
                        lhsT = a_words[:, g, 2 * P * t : 2 * P * (t + 1)].bitcast(FP4X4)
                        lhsT_scale = a_scales[:, g, cols]
                    else:
                        lhsT = quad_words[:, g, cols].bitcast(FP8X4)
                        lhsT_scale = quad_scales[:, g, cols]
                    nc.tensor.matmul_mx(
                        out=h_bank[i][:, t, :], lhsT=lhsT, lhsT_scale=lhsT_scale,
                        rhs=words[:, part].bitcast(FP8X4), rhs_scale=scales[:, part],
                        start=(c == 0), stop=(c == 3),
                    )

        def taper_h(i):
            h_rows[i] = work.tile([P, PACK, P], BF16, name="h_rows", bufs=4)
            for t in range(PACK):
                nc.scalar.activation(
                    out=h_rows[i][:, t, :], in_=h_bank[i][:, t, :], func=ACT.Identity,
                    scale=taper_col[:, t : t + 1], bias=bias_col[:, t : t + 1],
                )

        def group_h(i):
            copy = nc.scalar.copy if i in H_GROUPED_ON_SCALAR else nc.vector.tensor_copy
            h_grouped[i] = work.tile([P, P, PACK], BF16, name="h_grouped", bufs=4, align_bytes=64)
            copy(out=h_grouped[i][:], in_=h_rows[i][:].rearrange("p t m -> p m t"))

        def quantize_h(i):
            words = work.tile([P, P], U32, name="h_words", bufs=4, align_bytes=64)
            scales = work.tile([P, P], U8, name="h_scales", bufs=4, align_bytes=64)
            h_mx[i] = (words, scales)
            nc.vector.quantize_mx(
                out=words[:].bitcast(FP8X4), scales=scales[:], in_=h_grouped[i][:].rearrange("p m t -> p (m t)")
            )

        def stage2(i):
            words, scales = h_mx[i]
            s_banks[i] = []
            for g in range(2):
                cols = slice(GROUP * g, GROUP * (g + 1))
                dst = bank()
                nc.tensor.matmul_mx(
                    out=dst[:].rearrange("p a m -> p (a m)"),
                    lhsT=words[:].bitcast(FP8X4), lhsT_scale=scales[:],
                    rhs=c_words[:, cols].bitcast(FP8X4), rhs_scale=c_scales[:, cols],
                    start=True, stop=True,
                )
                s_banks[i].append(dst)

        def shift_s(i):
            shifted[i] = work.tile([P, DIRS], F32, name="shifted")
            for g in range(2):
                cols = slice(GROUP * g, GROUP * (g + 1))
                nc.vector.scalar_tensor_tensor(
                    out=shifted[i][:, cols], in0=s_banks[i][g][:].rearrange("p a m -> p (a m)"),
                    scalar=level_col[:, i : i + 1], in1=floor_all[:, cols], op0=ALU.mult, op1=ALU.add,
                )

        def parts(i):
            return HALVES if i == LAST else BOTH

        def gain_y(i):
            y_f32[i] = work.tile([P, DIRS], F32, name="y_f32", bufs=6)
            for lo, hi in parts(i):
                cols = slice(GROUP * lo, GROUP * hi)
                nc.vector.tensor_tensor(
                    out=y_f32[i][:, cols], in0=shifted[i][:, cols], in1=gain_all[:, cols], op=ALU.mult
                )
                nc.sync.dma_start(out=out_0[P * i : P * (i + 1), cols], in_=y_f32[i][:, cols])

        def round_y(i):
            copy = nc.vector.tensor_copy if i == LAST else nc.scalar.copy
            y_bf16[i] = work.tile([P, 2, 2 * P, 2], BF16, name="y_bf16", bufs=4)
            src = y_f32[i][:].rearrange("m (w u e) -> m u w e", u=2, e=2)
            for lo, hi in parts(i):
                copy(out=y_bf16[i][:, :, P * lo : P * hi, :], in_=src[:, :, P * lo : P * hi, :])

        def turn_y(i):
            words = y_bf16[i][:].rearrange("m u w e -> m u (w e)").bitcast(F32)
            for lo, hi in parts(i):
                y_bank[i, lo] = bank()
                for g in range(lo, hi):
                    for u in range(2):
                        nc.tensor.transpose(
                            y_bank[i, lo][:, 2 * g + u, :], words[:, u, P * g : P * (g + 1)], ident[:]
                        )

        def copy_y(i):
            if i % 2 == 0:
                y_grouped[i // 2] = work.tile([P, 2, 2 * P, PACK], BF16, name="y_grouped", align_bytes=64)
            windows = slice(P * (i % 2), P * (i % 2 + 1))
            for lo, hi in parts(i):
                nc.scalar.copy(
                    out=y_grouped[i // 2][:, lo:hi, windows, :].bitcast(F32),
                    in_=y_bank[i, lo][:, 2 * lo : 2 * hi, :].rearrange("p (g u) m -> p g m u", u=2),
                )

        def store_scales(first, last, queues):
            for q in range(4):
                queues[q % len(queues)].dma_start(
                    out=out_2[:, 4 * q : 4 * q + 4, first:last].rearrange("g r m -> r g m").bitcast(I32),
                    in_=y_scales[32 * q : 32 * q + 4, :, first:last].bitcast(I32),
                )

        def quantize_y(i):
            if i % 2 == 0:
                return
            windows = slice(P * (i - 1), P * (i + 1))
            for lo, hi in parts(i):
                for g in range(lo, hi):
                    nc.vector.quantize_mx(
                        out=y_words[:, g, windows].bitcast(FP8X4), scales=y_scales[:, g, windows],
                        in_=y_grouped[i // 2][:, g].rearrange("p m t -> p (m t)"),
                    )
                nc.sync.dma_start(
                    out=out_1.rearrange("g p m t -> p g (m t)").bitcast(I32)[:, lo:hi, windows],
                    in_=y_words[:, lo:hi, windows].bitcast(I32),
                )
            if windows.stop == EARLY_SCALES:
                store_scales(0, EARLY_SCALES, [nc.sync])
            if i == LAST:
                store_scales(EARLY_SCALES, WINDOWS, [nc.sync, nc.scalar])


        make_identity(nc, ident[:])
        nc.gpsimd.memset(level_rows[:], 0.0)
        nc.vector.memset(scales_in[:].bitcast(I32), 0)

        load_cov(0)
        load_scale_rows(scales_in[:, : 2 * LAGS], avg_scales)
        load_quad(0)
        load_quad(1)
        nc.sync.dma_start(out=floor_in[:], in_=floor.rearrange("(n j) -> n j", n=P))
        nc.sync.dma_start(out=gain_in[:], in_=gain.rearrange("(n j) -> n j", n=P))
        nc.sync.dma_start(out=a_in[:].bitcast(I32), in_=avg_words.rearrange("g p b -> p g b").bitcast(I32))
        nc.sync.dma_start(out=taper_in[:], in_=taper.rearrange("(p t) -> p t", t=PACK))
        load_cov(1)
        nc.sync.dma_start(out=level_in[:], in_=level.rearrange("(i m) -> i m", m=P))
        load_cov(2)
        nc.sync.dma_start(out=offset_in[:], in_=offset.rearrange("(p t) -> p t", t=PACK))
        load_cov(3)
        load_cov(4)

        order_a_scales()
        turn_cov(0)
        copy_cov(0)
        group_quad(0, nc.vector.tensor_copy)
        quantize_cov(0)
        floor_turned = turn_vector(floor_in)
        quantize_quad(0)
        order_a_words()
        group_quad(1, nc.scalar.copy)
        gain_turned = turn_vector(gain_in)
        quantize_quad(1)
        copy_vector(floor_all, floor_turned, nc.vector.tensor_copy)
        nc.vector.tensor_copy(out=taper_col[:], in_=taper_in[:])
        nc.vector.tensor_tensor(out=bias_col[:], in0=offset_in[:], in1=taper_in[:], op=ALU.mult)

        def finish_gain():
            copy_vector(gain_all, gain_turned, nc.scalar.copy)
            nc.vector.tensor_copy(out=level_rows[:TILES, :], in_=level_in[:])

        def load_c():
            nc.sync.dma_start(
                out=c_words[:].bitcast(I32), in_=cos_words[0].rearrange("p n t -> p (n t)").bitcast(I32)
            )
            load_scale_rows(c_scales, cos_scales)

        def turn_level():
            turned = bank()
            nc.tensor.transpose(turned[:, 0, :], level_rows[:], ident[:])
            nc.scalar.copy(out=level_col[:], in_=turned[:, 0, :TILES])

        stages = [
            (round_y, -4), (load_cov, 5), (turn_y, -5), (taper_h, -1), (turn_cov, 1), (quantize_y, -6),
            (stage2, -2), (group_h, -1), (stage1, 0), (copy_cov, 1), (shift_s, -2), (quantize_h, -1),
            (quantize_cov, 1), (copy_y, -5), (gain_y, -2),
        ]
        once = {(0, quantize_cov): finish_gain, (1, turn_cov): load_c, (2, turn_cov): turn_level}
        steps = TILES - min(lead for stage, lead in stages)
        for s in range(steps):
            for stage, lead in stages:
                if 0 <= s + lead < TILES:
                    stage(s + lead)
                if (s, stage) in once:
                    once[s, stage]()
